import numpy as np, ml_dtypes
CORES = [2,10,50,58,66,74,122]
N = 7
CAP = 1024
T = N * CAP
def entries(a): return a.T.reshape(-1)
def pack(v, P): return np.ascontiguousarray(np.asarray(v, np.int32).reshape(-1, P).T)
def lists(rng, how):
    C = rng.integers(0, CAP + 1, (N, N))
    if how == "edge": C = np.array([0, 1, CAP - 1, CAP])[(rng.permutation(N)[:, None] + rng.permutation(N)[None, :]) % 4]
    if how == "full": C[:] = CAP
    if how == "lone": z = int(rng.integers(N)); k = C[z].copy(); C[:] = 0; C[z] = np.maximum(k, 1)
    if how == "none": u, v, w = rng.permutation(N)[:3]; C = np.maximum(C, 1); C[u] = 0; C[:, u] = 0; C[v] = 0; C[:, w] = 0
    if how == "zeros": C = rng.integers(4, CAP, (N, N))
    return {"cnt": np.stack([pack(np.concatenate([c, np.zeros(32 - N, np.int64)]), 16) for c in C])}
def setup_inputs(rng):
    return dict({"x": rng.standard_normal((N, 128, T), dtype=np.float32).astype(ml_dtypes.bfloat16)}, **lists(rng, "uniform"))
def setup_inputs_edge(rng):
    d = setup_inputs(rng); d.update(lists(rng, "edge"))
    for k in ("x",): d[k] = (d[k].astype(np.float32) * 1048576.0).astype(d[k].dtype)
    return d
def setup_inputs_full(rng):
    d = setup_inputs(rng); d.update(lists(rng, "full"))
    for k in ("x",): d[k] = (d[k].astype(np.float32) * (1 / 1024.0)).astype(d[k].dtype)
    return d
def setup_inputs_lone(rng):
    d = setup_inputs(rng); d.update(lists(rng, "lone"))
    return d
def setup_inputs_none(rng):
    d = setup_inputs(rng); d.update(lists(rng, "none"))
    return d
def setup_inputs_zeros(rng):
    d = setup_inputs(rng); d.update(lists(rng, "zeros"))
    K = np.stack([entries(a) for a in d["cnt"]])[:, :N]; B = np.cumsum(K, axis=1) - K
    Z = np.concatenate([B, B + rng.integers(2, K - 1), B + K - 1], axis=1)
    for r in range(N): d["x"][r][:, Z[r]] = 0
    d["x"][:, 0][rng.random((N, T)) < 0.5] = 0
    return d
def check_inputs(x):
    bad = []
    if x["cnt"].min() < 0 or x["cnt"].max() >= CAP + 1: bad.append("cnt out of range")
    if any(entries(a)[N:].any() for a in x["cnt"]): bad.append("an entry from N on isn't 0")
    return bad
def reference(x, cnt):
    C = np.stack([entries(c)[:N] for c in cnt]); S = np.cumsum(C, axis=1) - C
    y = np.zeros((N, 128, T), x.dtype)
    for d in range(N):
        got = np.concatenate([x[r][:, S[r, d]:S[r, d] + C[r, d]] for r in range(N)], axis=1); y[d][:, :got.shape[1]] = got
    return {"y": y}

from concourse.bass import DstId, RemoteDMATransfer
from concourse.mybir import AluOpType, ActivationFunctionType

N = 7
CAP = 1024
COLS = N * CAP
HALF = CAP // 2
XB = (N - 1) * CAP
ZB = XB + COLS
WEND = ZB + 8
K = CAP // 16
HK = K // 2
BIG = 60000.0
XCH = [0, 2048, 4096, 6144, 7168]

PLAN = [
    ([6, 1, 3], [5, 2, 4]),
    ([5, 0, 2], [4, 3, 6]),
    ([3, 4, 5, 1], [6, 0]),
    ([5, 0, 4], [1, 2, 6]),
    ([2, 6, 5], [3, 0, 1]),
    ([1, 3, 2, 6], [0, 4]),
    ([4, 0, 3], [2, 1, 5]),
]

SCRATCH = {
    "win": ("sbuf", [128, WEND], "bfloat16"),
    "sb": ("sbuf", [128, (N - 1) * CAP], "bfloat16"),
    "yb": ("sbuf", [128, COLS], "bfloat16"),
    "hb": ("sbuf", [128, 4 * CAP], "bfloat16"),
    "cs": ("sbuf", [1, 16], "int32"),
    "pb": ("sbuf", [128, 16], "int32"),
    "cf": ("sbuf", [128, 16], "float32"),
    "ones": ("sbuf", [128, N * K], "float32"),
    "sx": ("sbuf", [128, 16], "float32"),
    "pi": ("sbuf", [128, 1], "int32"),
    "qi": ("sbuf", [128, 1], "int32"),
    "bi": ("sbuf", [128, 1], "int32"),
    "qf": ("sbuf", [128, 1], "float32"),
    "bf": ("sbuf", [128, 1], "float32"),
    "j16": ("sbuf", [128, N * K], "float32"),
    "q16": ("sbuf", [128, 128], "float32"),
    "bk": ("sbuf", [8, 128], "float32"),
    "m16": ("sbuf", [128, 128], "float32"),
    "w1": ("sbuf", [8, 128], "float32"),
    "w2": ("sbuf", [8, 128], "float32"),
    "col": ("sbuf", [128, 16], "float32"),
    "rci": ("sbuf", [8, 2], "int32"),
    "rcf": ("sbuf", [8, 1], "float32"),
    "lm": ("sbuf", [128, 128], "float32"),
    "ind": ("sbuf", [128, N * K], "float32"),
    "lsts": ("sbuf", [128, N * K], "uint16"),
    "lstr": ("sbuf", [128, N * K], "uint16"),
    "pa": ("psum", [128, 512], "float32"),
    "pd": ("psum", [128, 512], "float32"),
    "cd": ("dram", [128, 2], "int32"),
    "hc": ("dram", [128, 2], "int32"),
    "cr": ("dram", [N, 128, 2], "int32"),
}
SEMAPHORES = (["ldc", "ldd", "ldo", "i1", "i2", "i3", "i4", "pbs", "v", "sl", "sent", "carr", "hcin", "rcl", "rcs",
               "kc", "pe1", "mm", "pe2", "rl", "st"]
              + ["x%d" % i for i in range(4)] + ["ga%d" % i for i in range(N)] + ["arr%d" % i for i in range(N)]
              + ["yk%d" % i for i in range(N)] + ["hin%d" % i for i in range(4)])


def engines(mask):
    return bin(mask).count("1")


def helper_of(topo, cores, r):
    me = cores[r]
    for h in range(128):
        if (h not in cores and topo.chip(h) == topo.chip(me) and topo.die(h) != topo.die(me)
                and all(topo.may_write(h, cores[d]) for d in range(N) if d != r)):
            return h
    return None


def send_counts(g, T, topo, src_core, src, dests, r):
    cores = T.cores
    if not dests:
        return 0
    ids = []
    mask = topo.mask(src_core, cores[dests[0]])
    for d in dests:
        mask = mask & topo.mask(src_core, cores[d])
        rid, pid, _se = topo.addr(cores[d])
        ids.append(DstId(rid=rid, pnc=pid))
    g.remote_dma_fused([RemoteDMATransfer(dst_ids=ids, dma_engine_mask=mask, remote_sem=T.sem.carr, srcs=[src],
                                          dsts=[T.cr[r] for _d in dests])], local_sem=T.sem.sent)
    return engines(mask)


def send(g, T, topo, src_core, dst_core, out, in_, sem, mask):
    rid, pid, _se = topo.addr(dst_core)
    g.remote_dma(out_ap=out, in_ap=in_, remote_sem=sem, local_sem=T.sem.sent, pid=pid, routing_id=rid,
                 dma_engine_mask=mask)
    return engines(mask)


def slot_of(me, r):
    return r if r < me else r - 1


def rank_program(g, core, T, topo):
    cores = list(T.cores)
    rank = T.rank_of(core)
    if rank is None:
        for r in range(N):
            if helper_of(topo, cores, r) == core:
                helper_program(g, core, r, cores, T, topo)
        return
    me_program(g, core, rank, cores, T, topo)


def off_mask(topo, cores, r):
    m = 0
    for d in range(N):
        if d != r:
            m = m | topo.mask(cores[r], cores[d])
    return m


def helper_program(g, core, r, cores, T, topo):
    dests = PLAN[r][1]
    if not dests:
        return
    ne = engines(topo.mask(cores[r], core) & ~off_mask(topo, cores, r))
    sent = 0
    g.wait_ge(T.sem.hcin, ne)
    sent += send_counts(g, T, topo, core, T.hc[:], dests, r)
    for i, d in enumerate(dests):
        g.wait_ge(T.sem["hin%d" % i], ne)
        s = slot_of(d, r) * CAP
        sent += send(g, T, topo, core, cores[d], T.win[:, s:s + CAP], T.hb[:, i * CAP:(i + 1) * CAP],
                     T.sem["arr%d" % r], topo.mask(core, cores[d]))
    g.wait_ge(T.sem.sent, sent)


def last_hop(topo, cores, src, dst):
    if dst in PLAN[src][0]:
        return cores[src], PLAN[src][0]
    return helper_of(topo, cores, src), PLAN[src][1]


def me_program(g, core, me, cores, T, topo):
    A = AluOpType
    sem = T.sem
    V = g.vector
    S = g.scalar
    P = g.tensor
    others = [r for r in range(N) if r != me]
    direct, viah = PLAN[me]
    helper = helper_of(topo, cores, me)
    spare = topo.mask(core, helper) & ~off_mask(topo, cores, me)

    order = []
    for i in range(max(len(direct), len(viah))):
        if i < len(viah):
            order.append((viah[i], 1, i))
        if i < len(direct):
            order.append((direct[i], 0, i))

    def xch(d):
        return [i for i in range(4) if XCH[i] < (d + 1) * CAP]

    g.sync.dma_start(T.cs[0:1, 0:16], T.cnt[0:8, :]).then_inc(sem.ldc, 16)
    for i in range(4):
        a, b = XCH[i], XCH[i + 1]
        g.sync.dma_start(T.win[:, XB + a:XB + b], T.x[:, a:b]).then_inc(sem["x%d" % i], 16)
    for i in range(8):
        S.dma_start(T.cd[16 * i:16 * i + 16, :], T.cnt[:, :]).then_inc(sem.ldd, 16)
    S.dma_start(T.cr[me, 0:16, :], T.cnt[:, :]).then_inc(sem.ldo, 16)

    g.iota(T.pi[:, 0:1], [[0, 1]], 0, 1).then_inc(sem.i1, 1)
    g.iota(T.q16[:], [[0, 8], [1, 16]], 0, 0, allow_small_or_imprecise_dtypes=True).then_inc(sem.i2, 1)
    g.iota(T.bk[:], [[1, 8], [0, 16]], 0, -1, allow_small_or_imprecise_dtypes=True).then_inc(sem.i3, 1)
    g.iota(T.j16[:], [[16, N * K]], 0, 0, allow_small_or_imprecise_dtypes=True).then_inc(sem.i4, 1)
    g.wait_ge(sem.ldc, 16)
    g.partition_broadcast(T.pb[:, 0:16], T.cs[0:1, 0:16], 128).then_inc(sem.pbs, 1)
    g.wait_ge(sem.ldd, 128)
    sent = 0
    if viah:
        sent += send(g, T, topo, core, helper, T.hc[:], T.cd[:], sem.hcin, spare)
    sent += send_counts(g, T, topo, core, T.cd[:], direct, me)
    for n, (d, lane, i) in enumerate(order):
        g.wait_ge(sem["ga%d" % n], 2)
        src = T.sb[:, n * CAP:(n + 1) * CAP]
        if lane:
            sent += send(g, T, topo, core, helper, T.hb[:, i * CAP:(i + 1) * CAP], src, sem["hin%d" % i], spare)
        else:
            s = slot_of(d, me) * CAP
            sent += send(g, T, topo, core, cores[d], T.win[:, s:s + CAP], src, sem["arr%d" % me],
                         topo.mask(core, cores[d]))
    g.wait_ge(sem.sent, sent)

    nv = [0]

    def v(ins):
        ins.then_inc(sem.v, 1)
        nv[0] += 1

    def vw():
        V.wait_ge(sem.v, nv[0])

    c = T.col
    v(V.memset(T.ones[:], 1.0))
    v(V.memset(T.win[:, ZB:WEND], 0.0))
    V.wait_ge(sem.i1, 1)
    v(V.tensor_scalar(T.qi[:], T.pi[:], 15, None, A.bitwise_and))
    v(V.tensor_scalar(T.bi[:], T.pi[:], 4, None, A.arith_shift_right))
    vw()
    v(V.tensor_copy(T.qf[:], T.qi[:]))
    v(V.tensor_copy(T.bf[:], T.bi[:]))
    vw()
    v(V.tensor_scalar(c[:, 0:1], T.bf[:], float(me), None, A.is_equal))
    v(V.tensor_scalar(c[:, 1:2], T.bf[:], float(me + 1), -1.0, A.is_equal, A.mult))
    v(V.tensor_scalar(c[:, 2:3], T.bf[:], 1.0, float(CAP), A.is_ge, A.mult))
    v(V.tensor_scalar(c[:, 3:4], T.bf[:], float(N), BIG, A.is_ge, A.mult))
    V.wait_ge(sem.i2, 1)
    v(V.tensor_scalar(T.m16[:], T.q16[:], T.qf[:, 0:1], None, A.is_equal))
    V.wait_ge(sem.i3, 1)
    V.tensor_scalar(T.w1[:], T.bk[:], 0.0, None, A.is_gt).then_inc(sem.kc, 1)
    V.tensor_scalar(T.w2[:], T.bk[:], 1.0, -1.0, A.is_equal, A.mult).then_inc(sem.kc, 1)
    vw()
    v(V.tensor_tensor(c[:, 4:5], c[:, 0:1], c[:, 1:2], A.add))
    v(V.tensor_tensor(c[:, 5:6], c[:, 2:3], c[:, 3:4], A.add))
    v(V.tensor_scalar(c[:, 6:7], c[:, 1:2], float(CAP), None, A.mult))
    vw()
    v(V.tensor_tensor(c[:, 7:8], c[:, 5:6], c[:, 6:7], A.add))
    v(V.tensor_scalar(c[:, 8:9], c[:, 4:5], float(XB - CAP * me), None, A.mult))
    vw()
    v(V.tensor_tensor(c[:, 9:10], c[:, 7:8], c[:, 8:9], A.add))
    V.wait_ge(sem.pbs, 1)
    v(V.tensor_copy(T.cf[:], T.pb[:]))
    vw()
    v(V.tensor_tensor_scan(T.sx[:], T.ones[:, 0:16], T.cf[:], 0.0, A.mult, A.add))
    vw()

    def s_col(d):
        return T.sx[:, 2 * d - 1:2 * d] if d else 0.0

    V.wait_ge(sem.i4, 1)
    for n, (d, lane, i) in enumerate(order):
        V.tensor_scalar(T.lsts[:, n * K:(n + 1) * K], T.j16[:, 0:K], T.qf[:, 0:1], s_col(d), A.add,
                        A.add).then_inc(sem.sl, 1)
    V.wait_ge(sem.sl, len(order))
    S.wait_ge(sem.sl, len(order))
    seen = set()
    for n, (d, lane, i) in enumerate(order):
        for ch in xch(d):
            if ch not in seen:
                seen.add(ch)
                V.wait_ge(sem["x%d" % ch], 16)
                S.wait_ge(sem["x%d" % ch], 16)
        win = T.win[:, XB:XB + (d + 1) * CAP]
        V.tensor_copy(T.sb[:, n * CAP:n * CAP + HALF],
                      win.indirect(T.lsts[:, n * K:n * K + HK])).then_inc(sem["ga%d" % n], 1)
        S.activation(T.sb[:, n * CAP + HALF:(n + 1) * CAP], win.indirect(T.lsts[:, n * K + HK:(n + 1) * K]),
                     ActivationFunctionType.Copy).then_inc(sem["ga%d" % n], 1)
    for ch in range(4):
        if ch not in seen:
            V.wait_ge(sem["x%d" % ch], 16)
            S.wait_ge(sem["x%d" % ch], 16)

    total = 0
    for r in others:
        cc, dests = last_hop(topo, cores, r, me)
        m = topo.mask(cc, cores[me])
        for d in dests:
            m = m & topo.mask(cc, cores[d])
        total += engines(m)
    g.sync.wait_ge(sem.ldo, 16)
    g.sync.wait_ge(sem.carr, total)
    g.sync.dma_start(T.rci[0:N, 0:2], T.cr[:, me, :]).then_inc(sem.rcl, 16)

    v(V.tensor_scalar(c[:, 10:11], c[:, 4:5], s_col(me), c[:, 9:10], A.mult, A.add))
    V.wait_ge(sem.rcl, 16)
    V.tensor_copy(T.rcf[0:N, :], T.rci[0:N, 0:1]).then_inc(sem.rcs, 1)

    P.wait_ge(sem.kc, 2)
    P.wait_ge(sem.rcs, 1)
    P.matmul(T.pd[:, 0:1], T.w1[0:N, :], T.rcf[0:N, :], True, True).then_inc(sem.pe1, 1)
    P.matmul(T.pd[:, 1:2], T.w2[0:N, :], T.rcf[0:N, :], True, True).then_inc(sem.pe1, 1)
    P.matmul(T.pa[:, 0:N * K], T.q16[0:1, :], T.ones[0:1, :], True, False)
    P.matmul(T.pa[:, 0:N * K], T.ones[0:1, 0:128], T.j16[0:1, :], False, False)
    P.wait_ge(sem.mm, 2)
    P.matmul(T.pa[:, 0:N * K], T.lm[:], T.ind[:], False, True).then_inc(sem.pe2, 1)

    V.wait_ge(sem.pe1, 2)
    vw()
    v(V.tensor_tensor(c[:, 11:12], T.pd[:, 1:2], c[:, 10:11], A.add))
    V.tensor_scalar(T.ind[:], T.j16[:], T.qf[:, 0:1], T.pd[:, 0:1], A.add, A.is_ge).then_inc(sem.mm, 1)
    vw()
    V.tensor_scalar(T.lm[:], T.m16[:], c[:, 11:12], None, A.mult).then_inc(sem.mm, 1)
    V.wait_ge(sem.pe2, 1)

    def wstart(k):
        for r in range(k, N):
            if r != me:
                return slot_of(me, r) * CAP
        return XB

    blocks = list(range(N - 1, -1, -1))
    for k in blocks:
        ws = wstart(k)
        V.tensor_scalar(T.lstr[:, k * K:(k + 1) * K], T.pa[:, k * K:(k + 1) * K], float(-ws), float(ZB - ws), A.add,
                        A.min).then_inc(sem.rl, 1)
    V.wait_ge(sem.rl, N)
    S.wait_ge(sem.rl, N)

    for k in blocks:
        if k != me:
            n = engines(topo.mask(last_hop(topo, cores, k, me)[0], core))
            V.wait_ge(sem["arr%d" % k], n)
            S.wait_ge(sem["arr%d" % k], n)
        win = T.win[:, wstart(k):WEND]
        V.tensor_copy(T.yb[:, k * CAP:k * CAP + HALF],
                      win.indirect(T.lstr[:, k * K:k * K + HK])).then_inc(sem["yk%d" % k], 1)
        S.activation(T.yb[:, k * CAP + HALF:(k + 1) * CAP], win.indirect(T.lstr[:, k * K + HK:(k + 1) * K]),
                     ActivationFunctionType.Copy).then_inc(sem["yk%d" % k], 1)
        g.sync.wait_ge(sem["yk%d" % k], 2)
        g.sync.dma_start(T.y[:, k * CAP:(k + 1) * CAP], T.yb[:, k * CAP:(k + 1) * CAP]).then_inc(sem.st, 16)
    g.sync.wait_ge(sem.st, 16 * N)
    V.wait_ge(sem.v, nv[0])
